import numpy as np
import ml_dtypes

BF16 = ml_dtypes.bfloat16


def bf(x):
    return np.asarray(x, np.float32).astype(BF16)


def f32(x):
    return np.asarray(x, np.float32)


def f64(x):
    return np.asarray(x).astype(np.float64)


def striped(idx):
    return np.tile(idx.reshape(-1, 16).T, (8, 1))


S, K, M, N = 256, 256, 512, 128


def setup_inputs():
    return {"table": bf(np.random.standard_normal((S, K))), "w": bf(np.random.standard_normal((K, M)) / np.sqrt(K)), "c": f32(0.2 + 0.8 * np.random.random_sample((1, N))), "offs": striped(np.sort(np.random.permutation(S)[:N]))}


def reference(table, w, c, offs):
    idx = offs[:16].T.reshape(-1)
    x = f64(table)[idx].T
    y = f64(w).T @ x
    return y * f64(c)

@@ -1,0 +1,80 @@
+import concourse.mybir as mybir
+from concourse.masks import make_identity
+
+P = 128
+S, K, M, N = 256, 256, 512, 128
+S_BLOCKS, K_BLOCKS, M_BLOCKS = S // P, K // P, M // P
+FLOPS = 2 * K * M * N
+BANK = 512
+WARM_UPS = 2
+
+BF16, F32, U16 = mybir.dt.bfloat16, mybir.dt.float32, mybir.dt.uint16
+
+
+def tile_gather_matmul_kernel(tc, table, w, c, offs, out):
+    nc = tc.nc
+    with tc.tile_pool(name="held", bufs=1) as held:
+        zeros = held.tile([P, P], BF16, name="zeros")
+        nc.gpsimd.memset(zeros[:], 0.0)
+        identity = held.tile([P, P], BF16, name="identity")
+        make_identity(nc, identity[:])
+        ones_row = held.tile([1, P], F32, name="ones_row")
+        nc.vector.memset(ones_row[:], 1.0)
+
+        queues = [nc.sync, nc.scalar]
+        tokens = [held.tile([P, K], BF16, name=f"tokens{s}") for s in range(S_BLOCKS)]
+        for s in range(S_BLOCKS):
+            queues[s].dma_start(tokens[s][:], table[s * P : (s + 1) * P, :])
+        score_row = held.tile([1, N], F32, name="score_row")
+        nc.sync.dma_start(score_row[:], c)
+        offsets = held.tile([P, N // 16], U16, name="offsets")
+        nc.sync.dma_start(offsets[:], offs)
+        weights = [held.tile([P, M], BF16, name=f"weights{k}") for k in range(K_BLOCKS)]
+        for k in range(K_BLOCKS):
+            queues[k].dma_start(weights[k][:], w[k * P : (k + 1) * P, :])
+
+        with tc.psum_pool(name="early", bufs=1) as early:
+            unread = early.tile([P, BANK // P, P], F32, name="unread")
+            for turn in range(WARM_UPS):
+                nc.tensor.matmul(
+                    unread[:],
+                    zeros[:],
+                    zeros[:].unsqueeze(1).to_broadcast([P, BANK // P, P]),
+                    start=True,
+                    stop=True,
+                )
+
+        with (
+            tc.psum_pool(name="sums", bufs=1) as sums,
+            tc.psum_pool(name="flip", bufs=S_BLOCKS * K_BLOCKS) as flip,
+        ):
+            features = [held.tile([P, S], BF16, name=f"features{k}") for k in range(K_BLOCKS)]
+            for k in range(K_BLOCKS):
+                for s in range(S_BLOCKS):
+                    flipped = flip.tile([P, P], BF16, name="flipped")
+                    nc.tensor.transpose(flipped[:], tokens[s][:, k * P : (k + 1) * P], identity[:])
+                    if s == 0:
+                        nc.vector.tensor_copy(features[k][:, s * P : (s + 1) * P], flipped[:])
+                    else:
+                        nc.scalar.copy(features[k][:, s * P : (s + 1) * P], flipped[:])
+
+            spread = flip.tile([P, N], F32, name="spread", tag="flipped")
+            nc.tensor.matmul(spread[:], ones_row[:], score_row[:], start=True, stop=True)
+            scores = held.tile([P, N], F32, name="scores")
+            nc.vector.tensor_copy(scores[:], spread[:])
+
+            banks = [sums.tile([P, N], F32, name=f"bank{m}") for m in range(M_BLOCKS)]
+            for k in range(K_BLOCKS):
+                for m in range(M_BLOCKS):
+                    nc.tensor.matmul(
+                        banks[m][:],
+                        weights[k][:, m * P : (m + 1) * P],
+                        features[k][:].indirect(offsets[:]),
+                        start=(k == 0),
+                        stop=(k == K_BLOCKS - 1),
+                    )
+
+            for m in range(M_BLOCKS):
+                scaled = held.tile([P, N], F32, name=f"scaled{m}")
+                nc.vector.tensor_tensor(scaled[:], banks[m][:], scores[:], mybir.AluOpType.mult)
+                queues[m % 2].dma_start(out[m * P : (m + 1) * P, :], scaled[:])

@@ -18,15 +18,16 @@ def tile_gather_matmul_kernel(tc, table, w, c, offs, out):
         nc.gpsimd.memset(zeros[:], 0.0)
         identity = held.tile([P, P], BF16, name="identity")
         make_identity(nc, identity[:])
-        ones_row = held.tile([1, P], F32, name="ones_row")
-        nc.vector.memset(ones_row[:], 1.0)
+        score_rows = held.tile([P, N], F32, name="score_rows")
+        nc.vector.memset(score_rows[:], 0.0)
+        ones = held.tile([P, P], F32, name="ones")
+        nc.vector.memset(ones[:], 1.0)
 
         queues = [nc.sync, nc.scalar]
         tokens = [held.tile([P, K], BF16, name=f"tokens{s}") for s in range(S_BLOCKS)]
         for s in range(S_BLOCKS):
             queues[s].dma_start(tokens[s][:], table[s * P : (s + 1) * P, :])
-        score_row = held.tile([1, N], F32, name="score_row")
-        nc.sync.dma_start(score_row[:], c)
+        nc.sync.dma_start(score_rows[0:1, :], c)
         offsets = held.tile([P, N // 16], U16, name="offsets")
         nc.sync.dma_start(offsets[:], offs)
         weights = [held.tile([P, M], BF16, name=f"weights{k}") for k in range(K_BLOCKS)]
@@ -59,22 +60,20 @@ def tile_gather_matmul_kernel(tc, table, w, c, offs, out):
                         nc.scalar.copy(features[k][:, s * P : (s + 1) * P], flipped[:])
 
             spread = flip.tile([P, N], F32, name="spread", tag="flipped")
-            nc.tensor.matmul(spread[:], ones_row[:], score_row[:], start=True, stop=True)
+            nc.tensor.matmul(spread[:], ones[:], score_rows[:], start=True, stop=True)
             scores = held.tile([P, N], F32, name="scores")
             nc.vector.tensor_copy(scores[:], spread[:])
 
-            banks = [sums.tile([P, N], F32, name=f"bank{m}") for m in range(M_BLOCKS)]
-            for k in range(K_BLOCKS):
-                for m in range(M_BLOCKS):
+            for m in range(M_BLOCKS):
+                bank = sums.tile([P, N], F32, name=f"bank{m}")
+                for k in range(K_BLOCKS):
                     nc.tensor.matmul(
-                        banks[m][:],
+                        bank[:],
                         weights[k][:, m * P : (m + 1) * P],
                         features[k][:].indirect(offsets[:]),
                         start=(k == 0),
                         stop=(k == K_BLOCKS - 1),
                     )
-
-            for m in range(M_BLOCKS):
                 scaled = held.tile([P, N], F32, name=f"scaled{m}")
-                nc.vector.tensor_tensor(scaled[:], banks[m][:], scores[:], mybir.AluOpType.mult)
+                nc.vector.tensor_tensor(scaled[:], bank[:], scores[:], mybir.AluOpType.mult)
                 queues[m % 2].dma_start(out[m * P : (m + 1) * P, :], scaled[:])

@@ -18,18 +18,17 @@ def tile_gather_matmul_kernel(tc, table, w, c, offs, out):
         nc.gpsimd.memset(zeros[:], 0.0)
         identity = held.tile([P, P], BF16, name="identity")
         make_identity(nc, identity[:])
-        score_rows = held.tile([P, N], F32, name="score_rows")
-        nc.vector.memset(score_rows[:], 0.0)
-        ones = held.tile([P, P], F32, name="ones")
-        nc.vector.memset(ones[:], 1.0)
+        identity_f32 = held.tile([P, P], F32, name="identity_f32")
+        nc.vector.tensor_copy(identity_f32[:], identity[:])
 
         queues = [nc.sync, nc.scalar]
         tokens = [held.tile([P, K], BF16, name=f"tokens{s}") for s in range(S_BLOCKS)]
         for s in range(S_BLOCKS):
             queues[s].dma_start(tokens[s][:], table[s * P : (s + 1) * P, :])
-        nc.sync.dma_start(score_rows[0:1, :], c)
         offsets = held.tile([P, N // 16], U16, name="offsets")
         nc.sync.dma_start(offsets[:], offs)
+        score_column = held.tile([N, 1], F32, name="score_column")
+        nc.scalar.dma_start(score_column[:], c.rearrange("o n -> n o"))
         weights = [held.tile([P, M], BF16, name=f"weights{k}") for k in range(K_BLOCKS)]
         for k in range(K_BLOCKS):
             queues[k].dma_start(weights[k][:], w[k * P : (k + 1) * P, :])
@@ -60,7 +59,7 @@ def tile_gather_matmul_kernel(tc, table, w, c, offs, out):
                         nc.scalar.copy(features[k][:, s * P : (s + 1) * P], flipped[:])
 
             spread = flip.tile([P, N], F32, name="spread", tag="flipped")
-            nc.tensor.matmul(spread[:], ones[:], score_rows[:], start=True, stop=True)
+            nc.tensor.transpose(spread[:], score_column[:].to_broadcast([N, P]), identity_f32[:])
             scores = held.tile([P, N], F32, name="scores")
             nc.vector.tensor_copy(scores[:], spread[:])
 

@@ -53,10 +53,7 @@ def tile_gather_matmul_kernel(tc, table, w, c, offs, out):
                 for s in range(S_BLOCKS):
                     flipped = flip.tile([P, P], BF16, name="flipped")
                     nc.tensor.transpose(flipped[:], tokens[s][:, k * P : (k + 1) * P], identity[:])
-                    if s == 0:
-                        nc.vector.tensor_copy(features[k][:, s * P : (s + 1) * P], flipped[:])
-                    else:
-                        nc.scalar.copy(features[k][:, s * P : (s + 1) * P], flipped[:])
+                    nc.vector.tensor_copy(features[k][:, s * P : (s + 1) * P], flipped[:])
 
             spread = flip.tile([P, N], F32, name="spread", tag="flipped")
             nc.tensor.transpose(spread[:], score_column[:].to_broadcast([N, P]), identity_f32[:])

@@ -4,6 +4,7 @@ from concourse.masks import make_identity
 P = 128
 S, K, M, N = 256, 256, 512, 128
 S_BLOCKS, K_BLOCKS, M_BLOCKS = S // P, K // P, M // P
+M_HALF = M // 2
 FLOPS = 2 * K * M * N
 BANK = 512
 WARM_UPS = 2
@@ -29,9 +30,12 @@ def tile_gather_matmul_kernel(tc, table, w, c, offs, out):
         nc.sync.dma_start(offsets[:], offs)
         score_column = held.tile([N, 1], F32, name="score_column")
         nc.scalar.dma_start(score_column[:], c.rearrange("o n -> n o"))
-        weights = [held.tile([P, M], BF16, name=f"weights{k}") for k in range(K_BLOCKS)]
-        for k in range(K_BLOCKS):
-            queues[k].dma_start(weights[k][:], w[k * P : (k + 1) * P, :])
+        weights = [held.tile([P, K_BLOCKS, M_HALF], BF16, name=f"weights{h}") for h in range(2)]
+        for h in range(2):
+            nc.sync.dma_start(
+                weights[h][:],
+                w[:, h * M_HALF : (h + 1) * M_HALF].rearrange("(k p) m -> p k m", p=P),
+            )
 
         with tc.psum_pool(name="early", bufs=1) as early:
             unread = early.tile([P, BANK // P, P], F32, name="unread")
@@ -65,7 +69,7 @@ def tile_gather_matmul_kernel(tc, table, w, c, offs, out):
                 for k in range(K_BLOCKS):
                     nc.tensor.matmul(
                         bank[:],
-                        weights[k][:, m * P : (m + 1) * P],
+                        weights[m * P // M_HALF][:, k, m * P % M_HALF : m * P % M_HALF + P],
                         features[k][:].indirect(offsets[:]),
                         start=(k == 0),
                         stop=(k == K_BLOCKS - 1),

@@ -4,7 +4,9 @@ from concourse.masks import make_identity
 P = 128
 S, K, M, N = 256, 256, 512, 128
 S_BLOCKS, K_BLOCKS, M_BLOCKS = S // P, K // P, M // P
-M_HALF = M // 2
+HALVES = 2
+M_HALF = M // HALVES
+BLOCKS_IN_HALF = M_HALF // P
 FLOPS = 2 * K * M * N
 BANK = 512
 WARM_UPS = 2
@@ -30,12 +32,15 @@ def tile_gather_matmul_kernel(tc, table, w, c, offs, out):
         nc.sync.dma_start(offsets[:], offs)
         score_column = held.tile([N, 1], F32, name="score_column")
         nc.scalar.dma_start(score_column[:], c.rearrange("o n -> n o"))
-        weights = [held.tile([P, K_BLOCKS, M_HALF], BF16, name=f"weights{h}") for h in range(2)]
-        for h in range(2):
-            nc.sync.dma_start(
-                weights[h][:],
-                w[:, h * M_HALF : (h + 1) * M_HALF].rearrange("(k p) m -> p k m", p=P),
-            )
+        weights = [
+            [held.tile([P, M_HALF], BF16, name=f"weights{h}{k}") for k in range(K_BLOCKS)]
+            for h in range(HALVES)
+        ]
+        for h in range(HALVES):
+            for k in range(K_BLOCKS):
+                nc.sync.dma_start(
+                    weights[h][k][:], w[k * P : (k + 1) * P, h * M_HALF : (h + 1) * M_HALF]
+                )
 
         with tc.psum_pool(name="early", bufs=1) as early:
             unread = early.tile([P, BANK // P, P], F32, name="unread")
@@ -64,16 +69,19 @@ def tile_gather_matmul_kernel(tc, table, w, c, offs, out):
             scores = held.tile([P, N], F32, name="scores")
             nc.vector.tensor_copy(scores[:], spread[:])
 
-            for m in range(M_BLOCKS):
-                bank = sums.tile([P, N], F32, name=f"bank{m}")
+            for h in range(HALVES):
+                banks = [sums.tile([P, N], F32, name=f"bank{h}{b}") for b in range(BLOCKS_IN_HALF)]
                 for k in range(K_BLOCKS):
-                    nc.tensor.matmul(
-                        bank[:],
-                        weights[m * P // M_HALF][:, k, m * P % M_HALF : m * P % M_HALF + P],
-                        features[k][:].indirect(offsets[:]),
-                        start=(k == 0),
-                        stop=(k == K_BLOCKS - 1),
-                    )
-                scaled = held.tile([P, N], F32, name=f"scaled{m}")
-                nc.vector.tensor_tensor(scaled[:], bank[:], scores[:], mybir.AluOpType.mult)
-                queues[m % 2].dma_start(out[m * P : (m + 1) * P, :], scaled[:])
+                    for b in range(BLOCKS_IN_HALF):
+                        nc.tensor.matmul(
+                            banks[b][:],
+                            weights[h][k][:, b * P : (b + 1) * P],
+                            features[k][:].indirect(offsets[:]),
+                            start=(k == 0),
+                            stop=(k == K_BLOCKS - 1),
+                        )
+                for b in range(BLOCKS_IN_HALF):
+                    m = h * BLOCKS_IN_HALF + b
+                    scaled = held.tile([P, N], F32, name=f"scaled{m}")
+                    nc.vector.tensor_tensor(scaled[:], banks[b][:], scores[:], mybir.AluOpType.mult)
+                    queues[m % 2].dma_start(out[m * P : (m + 1) * P, :], scaled[:])

@@ -69,19 +69,17 @@ def tile_gather_matmul_kernel(tc, table, w, c, offs, out):
             scores = held.tile([P, N], F32, name="scores")
             nc.vector.tensor_copy(scores[:], spread[:])
 
-            for h in range(HALVES):
-                banks = [sums.tile([P, N], F32, name=f"bank{h}{b}") for b in range(BLOCKS_IN_HALF)]
+            for m in range(M_BLOCKS):
+                h, b = divmod(m, BLOCKS_IN_HALF)
+                bank = sums.tile([P, N], F32, name=f"bank{m}")
                 for k in range(K_BLOCKS):
-                    for b in range(BLOCKS_IN_HALF):
-                        nc.tensor.matmul(
-                            banks[b][:],
-                            weights[h][k][:, b * P : (b + 1) * P],
-                            features[k][:].indirect(offsets[:]),
-                            start=(k == 0),
-                            stop=(k == K_BLOCKS - 1),
-                        )
-                for b in range(BLOCKS_IN_HALF):
-                    m = h * BLOCKS_IN_HALF + b
-                    scaled = held.tile([P, N], F32, name=f"scaled{m}")
-                    nc.vector.tensor_tensor(scaled[:], banks[b][:], scores[:], mybir.AluOpType.mult)
-                    queues[m % 2].dma_start(out[m * P : (m + 1) * P, :], scaled[:])
+                    nc.tensor.matmul(
+                        bank[:],
+                        weights[h][k][:, b * P : (b + 1) * P],
+                        features[k][:].indirect(offsets[:]),
+                        start=(k == 0),
+                        stop=(k == K_BLOCKS - 1),
+                    )
+                scaled = held.tile([P, N], F32, name=f"scaled{m}")
+                nc.vector.tensor_tensor(scaled[:], bank[:], scores[:], mybir.AluOpType.mult)
+                queues[m % 2].dma_start(out[m * P : (m + 1) * P, :], scaled[:])

@@ -8,8 +8,7 @@ HALVES = 2
 M_HALF = M // HALVES
 BLOCKS_IN_HALF = M_HALF // P
 FLOPS = 2 * K * M * N
-BANK = 512
-WARM_UPS = 2
+WARM_UPS, WARM_UP_WIDTH = 5, 256
 
 BF16, F32, U16 = mybir.dt.bfloat16, mybir.dt.float32, mybir.dt.uint16
 
@@ -17,8 +16,8 @@ BF16, F32, U16 = mybir.dt.bfloat16, mybir.dt.float32, mybir.dt.uint16
 def tile_gather_matmul_kernel(tc, table, w, c, offs, out):
     nc = tc.nc
     with tc.tile_pool(name="held", bufs=1) as held:
-        zeros = held.tile([P, P], BF16, name="zeros")
-        nc.gpsimd.memset(zeros[:], 0.0)
+        zero = held.tile([P, 1], BF16, name="zero")
+        nc.vector.memset(zero[:], 0.0)
         identity = held.tile([P, P], BF16, name="identity")
         make_identity(nc, identity[:])
         identity_f32 = held.tile([P, P], F32, name="identity_f32")
@@ -43,12 +42,12 @@ def tile_gather_matmul_kernel(tc, table, w, c, offs, out):
                 )
 
         with tc.psum_pool(name="early", bufs=1) as early:
-            unread = early.tile([P, BANK // P, P], F32, name="unread")
+            unread = early.tile([P, WARM_UP_WIDTH], F32, name="unread")
             for turn in range(WARM_UPS):
                 nc.tensor.matmul(
                     unread[:],
-                    zeros[:],
-                    zeros[:].unsqueeze(1).to_broadcast([P, BANK // P, P]),
+                    zero[:].to_broadcast([P, P]),
+                    zero[:].to_broadcast([P, WARM_UP_WIDTH]),
                     start=True,
                     stop=True,
                 )

@@ -41,6 +41,9 @@ def tile_gather_matmul_kernel(tc, table, w, c, offs, out):
                     weights[h][k][:], w[k * P : (k + 1) * P, h * M_HALF : (h + 1) * M_HALF]
                 )
 
+        unused = held.tile([P, 1], BF16, name="unused")
+        nc.scalar.copy(unused[:], zero[:])
+
         with tc.psum_pool(name="early", bufs=1) as early:
             unread = early.tile([P, WARM_UP_WIDTH], F32, name="unread")
             for turn in range(WARM_UPS):
@@ -61,7 +64,8 @@ def tile_gather_matmul_kernel(tc, table, w, c, offs, out):
                 for s in range(S_BLOCKS):
                     flipped = flip.tile([P, P], BF16, name="flipped")
                     nc.tensor.transpose(flipped[:], tokens[s][:, k * P : (k + 1) * P], identity[:])
-                    nc.vector.tensor_copy(features[k][:, s * P : (s + 1) * P], flipped[:])
+                    copy_out = [nc.vector.tensor_copy, nc.scalar.copy][s]
+                    copy_out(features[k][:, s * P : (s + 1) * P], flipped[:])
 
             spread = flip.tile([P, N], F32, name="spread", tag="flipped")
             nc.tensor.transpose(spread[:], score_column[:].to_broadcast([N, P]), identity_f32[:])

@@ -85,4 +85,4 @@ def tile_gather_matmul_kernel(tc, table, w, c, offs, out):
                     )
                 scaled = held.tile([P, N], F32, name=f"scaled{m}")
                 nc.vector.tensor_tensor(scaled[:], bank[:], scores[:], mybir.AluOpType.mult)
-                queues[m % 2].dma_start(out[m * P : (m + 1) * P, :], scaled[:])
+                queues[(m + 1) % 2].dma_start(out[m * P : (m + 1) * P, :], scaled[:])

import concourse.mybir as mybir
from concourse.masks import make_identity

P = 128
S, K, M, N = 256, 256, 512, 128
S_BLOCKS, K_BLOCKS, M_BLOCKS = S // P, K // P, M // P
HALVES = 2
M_HALF = M // HALVES
BLOCKS_IN_HALF = M_HALF // P
FLOPS = 2 * K * M * N
WARM_UPS, WARM_UP_WIDTH = 5, 256

BF16, F32, U16 = mybir.dt.bfloat16, mybir.dt.float32, mybir.dt.uint16


def tile_gather_matmul_kernel(tc, table, w, c, offs, out):
    nc = tc.nc
    with tc.tile_pool(name="held", bufs=1) as held:
        zero = held.tile([P, 1], BF16, name="zero")
        nc.vector.memset(zero[:], 0.0)
        identity = held.tile([P, P], BF16, name="identity")
        make_identity(nc, identity[:])
        identity_f32 = held.tile([P, P], F32, name="identity_f32")
        nc.vector.tensor_copy(identity_f32[:], identity[:])

        queues = [nc.sync, nc.scalar]
        tokens = [held.tile([P, K], BF16, name=f"tokens{s}") for s in range(S_BLOCKS)]
        for s in range(S_BLOCKS):
            queues[s].dma_start(tokens[s][:], table[s * P : (s + 1) * P, :])
        offsets = held.tile([P, N // 16], U16, name="offsets")
        nc.sync.dma_start(offsets[:], offs)
        score_column = held.tile([N, 1], F32, name="score_column")
        nc.scalar.dma_start(score_column[:], c.rearrange("o n -> n o"))
        weights = [
            [held.tile([P, M_HALF], BF16, name=f"weights{h}{k}") for k in range(K_BLOCKS)]
            for h in range(HALVES)
        ]
        for h in range(HALVES):
            for k in range(K_BLOCKS):
                nc.sync.dma_start(
                    weights[h][k][:], w[k * P : (k + 1) * P, h * M_HALF : (h + 1) * M_HALF]
                )

        unused = held.tile([P, 1], BF16, name="unused")
        nc.scalar.copy(unused[:], zero[:])

        with tc.psum_pool(name="early", bufs=1) as early:
            unread = early.tile([P, WARM_UP_WIDTH], F32, name="unread")
            for turn in range(WARM_UPS):
                nc.tensor.matmul(
                    unread[:],
                    zero[:].to_broadcast([P, P]),
                    zero[:].to_broadcast([P, WARM_UP_WIDTH]),
                    start=True,
                    stop=True,
                )

        with (
            tc.psum_pool(name="sums", bufs=1) as sums,
            tc.psum_pool(name="flip", bufs=S_BLOCKS * K_BLOCKS) as flip,
        ):
            features = [held.tile([P, S], BF16, name=f"features{k}") for k in range(K_BLOCKS)]
            for k in range(K_BLOCKS):
                for s in range(S_BLOCKS):
                    flipped = flip.tile([P, P], BF16, name="flipped")
                    nc.tensor.transpose(flipped[:], tokens[s][:, k * P : (k + 1) * P], identity[:])
                    copy_out = [nc.vector.tensor_copy, nc.scalar.copy][s]
                    copy_out(features[k][:, s * P : (s + 1) * P], flipped[:])

            spread = flip.tile([P, N], F32, name="spread", tag="flipped")
            nc.tensor.transpose(spread[:], score_column[:].to_broadcast([N, P]), identity_f32[:])
            scores = held.tile([P, N], F32, name="scores")
            nc.vector.tensor_copy(scores[:], spread[:])

            for m in range(M_BLOCKS):
                h, b = divmod(m, BLOCKS_IN_HALF)
                bank = sums.tile([P, N], F32, name=f"bank{m}")
                for k in range(K_BLOCKS):
                    nc.tensor.matmul(
                        bank[:],
                        weights[h][k][:, b * P : (b + 1) * P],
                        features[k][:].indirect(offsets[:]),
                        start=(k == 0),
                        stop=(k == K_BLOCKS - 1),
                    )
                scaled = held.tile([P, N], F32, name=f"scaled{m}")
                nc.vector.tensor_tensor(scaled[:], bank[:], scores[:], mybir.AluOpType.mult)
                queues[(m + 1) % 2].dma_start(out[m * P : (m + 1) * P, :], scaled[:])
